import numpy as np
import ml_dtypes


def mxq(x, axis, fmt="e4m3"):
    dtype, down = {"e4m3": (ml_dtypes.float8_e4m3fn, 7), "e5m2": (ml_dtypes.float8_e5m2, 14)}[fmt]
    v = np.moveaxis(np.asarray(x, np.float32).astype(ml_dtypes.bfloat16).astype(np.float64), axis, -1)
    blocks = v.reshape(v.shape[:-1] + (-1, 32))
    amax = np.abs(blocks).max(-1, keepdims=True)
    byte = np.maximum(np.where(amax > 0, np.frexp(amax)[1] - 1 + 127, 0) - down, 1)
    scale = np.exp2(byte - 127.0)
    codes = (blocks / scale).astype(np.float32).astype(dtype).astype(np.float64)
    return np.moveaxis((codes * scale).reshape(v.shape), -1, axis)


WIDE = False


def mx_kscale(k):
    if not WIDE:
        return np.ones(k)
    levels = np.array([10, -10, 5, -5, 0])
    if k % 512:
        return np.exp2(np.random.permutation(np.resize(levels, k // 32))).repeat(32)
    a = np.empty((k // 512, 16))
    for p in range(k // 512):
        a[p, :8] = np.random.permutation(np.resize(levels, 8))
        for g in range(8):
            far = levels[np.abs(levels - a[p, g]) >= 10]
            a[p, g + 8] = far[np.random.randint(len(far))]
    return np.exp2(a.ravel()).repeat(32)


def f64(x):
    return np.asarray(x).astype(np.float64)


def striped(idx):
    return np.tile(idx.reshape(-1, 16).T, (8, 1)).astype(np.uint16)


def unstriped(offs):
    return offs[:16].T.reshape(-1).astype(np.int64)


E2M1 = np.array([0.0, 0.5, 1.0, 1.5, 2.0, 3.0, 4.0, 6.0, -0.0, -0.5, -1.0, -1.5, -2.0, -3.0, -4.0, -6.0])


def pack_weight(w, fmt):
    k, n = w.shape
    w = f64(np.asarray(w, np.float32).astype(ml_dtypes.bfloat16)).reshape(k // 32, 32, n)
    amax = np.abs(w).max(1)
    if fmt == "e4m3":
        byte = np.frexp(amax)[1] - 1 + 127 - 7
    else:
        mant, ex = np.frexp(amax / 6.0)
        byte = np.where(mant > 0.5, ex, ex - 1) + 127
    byte = np.clip(np.where(amax > 0, byte, 1), 1, 254)
    scaled = (w * np.exp2(127.0 - byte)[:, None, :]).reshape(k, n).astype(np.float32)
    by_word = np.ascontiguousarray(scaled.reshape(k // 512, 128, 4, n).transpose(0, 1, 3, 2))
    if fmt == "e4m3":
        words = by_word.astype(ml_dtypes.float8_e4m3fn).view(np.uint8)
    else:
        c = by_word.astype(ml_dtypes.float4_e2m1fn).view(np.uint8) & 0xF
        words = (c[..., 0::2] | (c[..., 1::2] << 4)).reshape(k // 512, 128, 2 * n)
    return np.ascontiguousarray(words), np.ascontiguousarray(byte.astype(np.uint8).reshape(k // 512, 16, n))


def unpack_weight(words, scales, fmt):
    g, _, n = scales.shape
    words = np.ascontiguousarray(words).reshape(g, 128, n, -1)
    if fmt == "e4m3":
        vals = words.view(ml_dtypes.float8_e4m3fn).astype(np.float64)
    else:
        nib = np.empty((g, 128, n, 4), np.uint8)
        nib[..., 0::2] = words & 0xF
        nib[..., 1::2] = words >> 4
        vals = E2M1[nib]
    vals = vals * np.repeat(np.exp2(scales.astype(np.float64) - 127.0), 8, axis=1)[..., None]
    return vals.transpose(0, 1, 3, 2).reshape(g * 512, n)


def pack_table(v):
    words, scales = pack_weight(v, "e4m3")
    return np.concatenate([words.reshape(words.shape[0], -1), scales.reshape(scales.shape[0], -1)], axis=1)


def unpack_table(tab):
    g, t = tab.shape[0], tab.shape[1] // 528
    return unpack_weight(tab[:, :512 * t].reshape(g, 128, t, 4), tab[:, 512 * t:].reshape(g, 16, t), "e4m3")


def silu(v):
    return v / (1.0 + np.exp(-np.maximum(v, -700.0)))


K, M, T, S = 512, 128, 2048, 1024


def setup_inputs():
    n = np.random.standard_normal
    s = mx_kscale(K)[:, None]
    p_w4 = pack_weight(n((K, M)) / np.sqrt(K) / s, "e2m1")
    return {
        "tab": pack_table(n((K, T)) * s),
        "w4_words": p_w4[0],
        "w4_scales": p_w4[1],
        "w8": (n((K, M)) / np.sqrt(K) / s).astype(np.float32),
        "r": (n((1024, 128))).astype(np.float32),
        "offs": striped(np.random.permutation(T)[:S]),
    }


def reference(tab, w4_words, w4_scales, w8, r, offs):
    tab_ = unpack_table(tab)[:, unstriped(offs)]
    w4_ = unpack_weight(w4_words, w4_scales, "e2m1")
    w8_ = mxq(f64(w8), 0, "e4m3")
    y = tab_.T @ w4_
    u = tab_.T @ w8_
    y = silu(y) * u
    return f64(r) + y

@@ -1,0 +1,114 @@
+from contextlib import ExitStack
+
+import concourse.mybir as mybir
+
+K, M, T, S = 512, 128, 2048, 1024
+FLOPS = 2 * 2 * K * M * S
+
+F32 = mybir.dt.float32
+BF16 = mybir.dt.bfloat16
+I32 = mybir.dt.int32
+U32 = mybir.dt.uint32
+U16 = mybir.dt.uint16
+U8 = mybir.dt.uint8
+FP8X4 = mybir.dt.float8_e4m3fn_x4
+FP4X4 = mybir.dt.float4_e2m1fn_x4
+SILU = mybir.ActivationFunctionType.Silu
+MULT = mybir.AluOpType.mult
+ADD = mybir.AluOpType.add
+
+P = 128
+CHUNK = 256
+NCH = S // CHUNK
+NB = CHUNK // P
+
+
+def tile_list_tabglu_tm_res_kernel(tc, tab, w4_words, w4_scales, w8, r, offs, out):
+    nc = tc.nc
+    with ExitStack() as ctx:
+        keep = ctx.enter_context(tc.tile_pool(name="keep", bufs=1))
+        psum = ctx.enter_context(tc.psum_pool(name="psum", bufs=1))
+
+        lists = keep.tile([P, S // 16], U16, name="lists")
+        tab_words = keep.tile([P, T], I32, name="tab_words", align_bytes=64)
+        tab_scales = keep.tile([P, T // 4], I32, name="tab_scales", align_bytes=64)
+        g4_words = keep.tile([P, 2 * M], U8, name="g4_words", align_bytes=64)
+        g4_scales = keep.tile([P, M // 4], I32, name="g4_scales", align_bytes=64)
+        w8_raw = keep.tile([P, 4, M], F32, name="w8_raw", align_bytes=64)
+        w8_grouped = keep.tile([P, M, 4], BF16, name="w8_grouped", align_bytes=64)
+        w8_codes = keep.tile([P, M], U32, name="w8_codes", align_bytes=64)
+        w8_scales = keep.tile([P, M], U8, name="w8_scales", align_bytes=64)
+        picked_words = [keep.tile([P, CHUNK], U32, name="pw%d" % c, align_bytes=64) for c in range(NCH)]
+        picked_scales = keep.tile([P, S], U8, name="picked_scales", align_bytes=64)
+        res = [keep.tile([P, 2 * NB, M], F32, name="res%d" % h) for h in range(2)]
+        sil = [keep.tile([P, NB, M], F32, name="sil%d" % c) for c in range(NCH)]
+        prod = [keep.tile([P, NB, M], F32, name="prod%d" % c) for c in range(NCH)]
+        done = [keep.tile([P, NB, M], F32, name="done%d" % c) for c in range(NCH)]
+        e_bank = [psum.tile([P, NB, M], F32, name="e%d" % c) for c in range(NCH)]
+        u_bank = [psum.tile([P, NB, M], F32, name="u%d" % c) for c in range(NCH)]
+        warm = keep.tile([P, 1], F32, name="warm")
+
+        nc.vector.memset(tab_scales[:], 0)
+        nc.vector.memset(tab_words[:, 0:8], 0)
+        nc.vector.memset(w8_raw[:, 0, 0:8], 0.0)
+        for h in range(2):
+            nc.vector.memset(res[h][:, 0, 0:8], 0.0)
+        nc.gpsimd.memset(g4_scales[:], 0)
+        nc.gpsimd.memset(warm[:], 0.0)
+        nc.scalar.activation(warm[:], warm[:], SILU)
+        scale_rows = tab[0, 4 * P * T :].rearrange("(q t) -> q t", t=T).bitcast(I32)
+        w4_rows = w4_scales[0].bitcast(I32)
+        nc.sync.dma_start(out=lists[:], in_=offs)
+        nc.sync.dma_start(out=g4_words[:].bitcast(I32), in_=w4_words[0].bitcast(I32))
+        for q in range(4):
+            nc.sync.dma_start(out=tab_scales[32 * q : 32 * q + 4, :], in_=scale_rows[4 * q : 4 * q + 4, :])
+        nc.sync.dma_start(out=tab_words[:], in_=tab[0, : 4 * P * T].rearrange("(p t) -> p t", p=P).bitcast(I32))
+        nc.sync.dma_start(out=w8_raw[:], in_=w8.rearrange("(p j) n -> p j n", j=4))
+        for q in range(4):
+            nc.gpsimd.dma_start(out=g4_scales[32 * q : 32 * q + 4, :], in_=w4_rows[4 * q : 4 * q + 4, :])
+        for h in range(2):
+            nc.sync.dma_start(out=res[h][:], in_=r[h * 512 : (h + 1) * 512, :].rearrange("(b p) n -> p b n", p=P))
+
+        nc.vector.tensor_copy(out=picked_scales[:], in_=tab_scales[:].bitcast(U8).indirect(lists[:]))
+        nc.scalar.copy(out=w8_grouped[:], in_=w8_raw[:].rearrange("p j n -> p n j"))
+
+        def gather(c):
+            cols = slice(c * CHUNK // 16, (c + 1) * CHUNK // 16)
+            nc.vector.tensor_copy(out=picked_words[c][:], in_=tab_words[:].bitcast(U32).indirect(lists[:, cols]))
+
+        def gate(c):
+            for b in range(NB):
+                toks = slice(b * P, (b + 1) * P)
+                alltoks = slice(c * CHUNK + b * P, c * CHUNK + (b + 1) * P)
+                nc.tensor.matmul_mx(out=e_bank[c][:, b, :], lhsT=picked_words[c][:, toks].bitcast(FP8X4), lhsT_scale=picked_scales[:, alltoks], rhs=g4_words[:].bitcast(FP4X4), rhs_scale=g4_scales[:].bitcast(U8), start=True, stop=True)
+            nc.scalar.activation(sil[c][:], e_bank[c][:], SILU)
+
+        def up(c):
+            for b in range(NB):
+                toks = slice(b * P, (b + 1) * P)
+                alltoks = slice(c * CHUNK + b * P, c * CHUNK + (b + 1) * P)
+                nc.tensor.matmul_mx(out=u_bank[c][:, b, :], lhsT=picked_words[c][:, toks].bitcast(FP8X4), lhsT_scale=picked_scales[:, alltoks], rhs=w8_codes[:].bitcast(FP8X4), rhs_scale=w8_scales[:], start=True, stop=True)
+
+        def finish(c):
+            nc.vector.tensor_tensor(prod[c][:], sil[c][:], u_bank[c][:], MULT)
+            adder = nc.gpsimd if c < 2 else nc.vector
+            adder.tensor_tensor(done[c][:], prod[c][:], res[c // 2][:, c % 2 * NB : (c % 2 + 1) * NB, :], ADD)
+            nc.sync.dma_start(out=out[c * CHUNK : (c + 1) * CHUNK, :].rearrange("(b p) n -> p b n", p=P), in_=done[c][:])
+
+        gather(0)
+        gate(0)
+        gather(1)
+        gate(1)
+        nc.vector.quantize_mx(out=w8_codes[:].bitcast(FP8X4), scales=w8_scales[:], in_=w8_grouped[:].rearrange("p n j -> p (n j)"))
+        up(0)
+        up(1)
+        gather(2)
+        gate(2)
+        up(2)
+        finish(0)
+        gather(3)
+        gate(3)
+        up(3)
+        finish(1)
+        finish(2)
+        finish(3)

@@ -18,9 +18,9 @@ MULT = mybir.AluOpType.mult
 ADD = mybir.AluOpType.add
 
 P = 128
-CHUNK = 256
-NCH = S // CHUNK
-NB = CHUNK // P
+PIECES = (8,)
+SPIECES = (4, 2, 2)
+GROUPS = ((0, 4), (4, 2), (6, 1), (7, 1))
 
 
 def tile_list_tabglu_tm_res_kernel(tc, tab, w4_words, w4_scales, w8, r, offs, out):
@@ -38,77 +38,97 @@ def tile_list_tabglu_tm_res_kernel(tc, tab, w4_words, w4_scales, w8, r, offs, ou
         w8_grouped = keep.tile([P, M, 4], BF16, name="w8_grouped", align_bytes=64)
         w8_codes = keep.tile([P, M], U32, name="w8_codes", align_bytes=64)
         w8_scales = keep.tile([P, M], U8, name="w8_scales", align_bytes=64)
-        picked_words = [keep.tile([P, CHUNK], U32, name="pw%d" % c, align_bytes=64) for c in range(NCH)]
-        picked_scales = keep.tile([P, S], U8, name="picked_scales", align_bytes=64)
-        res = [keep.tile([P, 2 * NB, M], F32, name="res%d" % h) for h in range(2)]
-        sil = [keep.tile([P, NB, M], F32, name="sil%d" % c) for c in range(NCH)]
-        prod = [keep.tile([P, NB, M], F32, name="prod%d" % c) for c in range(NCH)]
-        done = [keep.tile([P, NB, M], F32, name="done%d" % c) for c in range(NCH)]
-        e_bank = [psum.tile([P, NB, M], F32, name="e%d" % c) for c in range(NCH)]
-        u_bank = [psum.tile([P, NB, M], F32, name="u%d" % c) for c in range(NCH)]
+        picked_words = [keep.tile([P, n * P], U32, name="pw%d" % i, align_bytes=64) for i, n in enumerate(PIECES)]
+        picked_scales = [keep.tile([P, n * P], U8, name="ps%d" % i, align_bytes=64) for i, n in enumerate(SPIECES)]
+        res = [keep.tile([P, 4, M], F32, name="res%d" % h) for h in range(2)]
+        sil = [keep.tile([P, n, M], F32, name="sil%d" % i) for i, (b, n) in enumerate(GROUPS)]
+        prod = [keep.tile([P, n, M], F32, name="prod%d" % i) for i, (b, n) in enumerate(GROUPS)]
+        done = [keep.tile([P, n, M], F32, name="done%d" % i) for i, (b, n) in enumerate(GROUPS)]
+        e_bank = [psum.tile([P, n, M], F32, name="e%d" % i) for i, (b, n) in enumerate(GROUPS)]
+        u_bank = [psum.tile([P, n, M], F32, name="u%d" % i) for i, (b, n) in enumerate(GROUPS)]
         warm = keep.tile([P, 1], F32, name="warm")
 
+        scale_rows = tab[0, 4 * P * T :].rearrange("(q t) -> q t", t=T).bitcast(I32)
+        w4_rows = w4_scales[0].bitcast(I32)
+
+        nc.gpsimd.memset(g4_scales[:], 0)
         nc.vector.memset(tab_scales[:], 0)
-        nc.vector.memset(tab_words[:, 0:8], 0)
         nc.vector.memset(w8_raw[:, 0, 0:8], 0.0)
         for h in range(2):
             nc.vector.memset(res[h][:, 0, 0:8], 0.0)
-        nc.gpsimd.memset(g4_scales[:], 0)
-        nc.gpsimd.memset(warm[:], 0.0)
+        nc.vector.memset(warm[:], 0.0)
         nc.scalar.activation(warm[:], warm[:], SILU)
-        scale_rows = tab[0, 4 * P * T :].rearrange("(q t) -> q t", t=T).bitcast(I32)
-        w4_rows = w4_scales[0].bitcast(I32)
         nc.sync.dma_start(out=lists[:], in_=offs)
-        nc.sync.dma_start(out=g4_words[:].bitcast(I32), in_=w4_words[0].bitcast(I32))
-        for q in range(4):
-            nc.sync.dma_start(out=tab_scales[32 * q : 32 * q + 4, :], in_=scale_rows[4 * q : 4 * q + 4, :])
         nc.sync.dma_start(out=tab_words[:], in_=tab[0, : 4 * P * T].rearrange("(p t) -> p t", p=P).bitcast(I32))
-        nc.sync.dma_start(out=w8_raw[:], in_=w8.rearrange("(p j) n -> p j n", j=4))
         for q in range(4):
             nc.gpsimd.dma_start(out=g4_scales[32 * q : 32 * q + 4, :], in_=w4_rows[4 * q : 4 * q + 4, :])
+            nc.sync.dma_start(out=tab_scales[32 * q : 32 * q + 4, :], in_=scale_rows[4 * q : 4 * q + 4, :])
+        nc.sync.dma_start(out=w8_raw[:], in_=w8.rearrange("(p j) n -> p j n", j=4))
+        nc.sync.dma_start(out=g4_words[:].bitcast(I32), in_=w4_words[0].bitcast(I32))
         for h in range(2):
             nc.sync.dma_start(out=res[h][:], in_=r[h * 512 : (h + 1) * 512, :].rearrange("(b p) n -> p b n", p=P))
 
-        nc.vector.tensor_copy(out=picked_scales[:], in_=tab_scales[:].bitcast(U8).indirect(lists[:]))
         nc.scalar.copy(out=w8_grouped[:], in_=w8_raw[:].rearrange("p j n -> p n j"))
 
-        def gather(c):
-            cols = slice(c * CHUNK // 16, (c + 1) * CHUNK // 16)
-            nc.vector.tensor_copy(out=picked_words[c][:], in_=tab_words[:].bitcast(U32).indirect(lists[:, cols]))
+        def gather(i):
+            first = sum(PIECES[:i])
+            cols = slice(first * P // 16, (first + PIECES[i]) * P // 16)
+            nc.vector.tensor_copy(out=picked_words[i][:], in_=tab_words[:].bitcast(U32).indirect(lists[:, cols]))
 
-        def gate(c):
-            for b in range(NB):
-                toks = slice(b * P, (b + 1) * P)
-                alltoks = slice(c * CHUNK + b * P, c * CHUNK + (b + 1) * P)
-                nc.tensor.matmul_mx(out=e_bank[c][:, b, :], lhsT=picked_words[c][:, toks].bitcast(FP8X4), lhsT_scale=picked_scales[:, alltoks], rhs=g4_words[:].bitcast(FP4X4), rhs_scale=g4_scales[:].bitcast(U8), start=True, stop=True)
-            nc.scalar.activation(sil[c][:], e_bank[c][:], SILU)
+        def gather_scales(i):
+            first = sum(SPIECES[:i])
+            cols = slice(first * P // 16, (first + SPIECES[i]) * P // 16)
+            nc.vector.tensor_copy(out=picked_scales[i][:], in_=tab_scales[:].bitcast(U8).indirect(lists[:, cols]))
 
-        def up(c):
-            for b in range(NB):
-                toks = slice(b * P, (b + 1) * P)
-                alltoks = slice(c * CHUNK + b * P, c * CHUNK + (b + 1) * P)
-                nc.tensor.matmul_mx(out=u_bank[c][:, b, :], lhsT=picked_words[c][:, toks].bitcast(FP8X4), lhsT_scale=picked_scales[:, alltoks], rhs=w8_codes[:].bitcast(FP8X4), rhs_scale=w8_scales[:], start=True, stop=True)
+        def quantise():
+            nc.vector.quantize_mx(out=w8_codes[:].bitcast(FP8X4), scales=w8_scales[:], in_=w8_grouped[:].rearrange("p n j -> p (n j)"))
 
-        def finish(c):
-            nc.vector.tensor_tensor(prod[c][:], sil[c][:], u_bank[c][:], MULT)
-            adder = nc.gpsimd if c < 2 else nc.vector
-            adder.tensor_tensor(done[c][:], prod[c][:], res[c // 2][:, c % 2 * NB : (c % 2 + 1) * NB, :], ADD)
-            nc.sync.dma_start(out=out[c * CHUNK : (c + 1) * CHUNK, :].rearrange("(b p) n -> p b n", p=P), in_=done[c][:])
+        def multiply(i, gate):
+            first, count = GROUPS[i]
+            for b in range(first, first + count):
+                piece = [x for x in range(len(PIECES)) if sum(PIECES[:x]) <= b][-1]
+                at = (b - sum(PIECES[:piece])) * P
+                codes = picked_words[piece][:, at : at + P].bitcast(FP8X4)
+                piece = [x for x in range(len(SPIECES)) if sum(SPIECES[:x]) <= b][-1]
+                at = (b - sum(SPIECES[:piece])) * P
+                scales = picked_scales[piece][:, at : at + P]
+                if gate:
+                    nc.tensor.matmul_mx(out=e_bank[i][:, b - first, :], lhsT=codes, lhsT_scale=scales, rhs=g4_words[:].bitcast(FP4X4), rhs_scale=g4_scales[:].bitcast(U8), start=True, stop=True)
+                else:
+                    nc.tensor.matmul_mx(out=u_bank[i][:, b - first, :], lhsT=codes, lhsT_scale=scales, rhs=w8_codes[:].bitcast(FP8X4), rhs_scale=w8_scales[:], start=True, stop=True)
+            if gate:
+                nc.scalar.activation(sil[i][:], e_bank[i][:], SILU)
+
+        def times(i):
+            nc.vector.tensor_tensor(prod[i][:], sil[i][:], u_bank[i][:], MULT)
+
+        def plus(i, engine):
+            first, count = GROUPS[i]
+            engine.tensor_tensor(done[i][:], prod[i][:], res[first // 4][:, first % 4 : first % 4 + count, :], ADD)
+
+        def store(i, engine=None):
+            first, count = GROUPS[i]
+            (engine or nc.sync).dma_start(out=out[first * P : (first + count) * P, :].rearrange("(b p) n -> p b n", p=P), in_=done[i][:])
 
         gather(0)
-        gate(0)
-        gather(1)
-        gate(1)
-        nc.vector.quantize_mx(out=w8_codes[:].bitcast(FP8X4), scales=w8_scales[:], in_=w8_grouped[:].rearrange("p n j -> p (n j)"))
-        up(0)
-        up(1)
-        gather(2)
-        gate(2)
-        up(2)
-        finish(0)
-        gather(3)
-        gate(3)
-        up(3)
-        finish(1)
-        finish(2)
-        finish(3)
+        gather_scales(0)
+        multiply(0, True)
+        quantise()
+        multiply(0, False)
+        gather_scales(1)
+        multiply(1, True)
+        multiply(1, False)
+        gather_scales(2)
+        for i in (2, 3):
+            multiply(i, True)
+            multiply(i, False)
+        times(0)
+        plus(0, nc.vector)
+        store(0)
+        times(1)
+        plus(1, nc.vector)
+        store(1)
+        for i in (2, 3):
+            times(i)
+            plus(i, nc.vector)
+            store(i)

@@ -18,9 +18,9 @@ MULT = mybir.AluOpType.mult
 ADD = mybir.AluOpType.add
 
 P = 128
-PIECES = (8,)
-SPIECES = (4, 2, 2)
-GROUPS = ((0, 4), (4, 2), (6, 1), (7, 1))
+PIECES = (2, 2, 2, 2)
+SPIECES = (8,)
+GROUPS = ((0, 2), (2, 2), (4, 2), (6, 1), (7, 1))
 
 
 def tile_list_tabglu_tm_res_kernel(tc, tab, w4_words, w4_scales, w8, r, offs, out):
@@ -44,8 +44,8 @@ def tile_list_tabglu_tm_res_kernel(tc, tab, w4_words, w4_scales, w8, r, offs, ou
         sil = [keep.tile([P, n, M], F32, name="sil%d" % i) for i, (b, n) in enumerate(GROUPS)]
         prod = [keep.tile([P, n, M], F32, name="prod%d" % i) for i, (b, n) in enumerate(GROUPS)]
         done = [keep.tile([P, n, M], F32, name="done%d" % i) for i, (b, n) in enumerate(GROUPS)]
-        e_bank = [psum.tile([P, n, M], F32, name="e%d" % i) for i, (b, n) in enumerate(GROUPS)]
-        u_bank = [psum.tile([P, n, M], F32, name="u%d" % i) for i, (b, n) in enumerate(GROUPS)]
+        e_bank = [psum.tile([P, n, M], F32, name="e%d" % i, tag="e%d" % (i % 3 if i < 4 else 3)) for i, (b, n) in enumerate(GROUPS)]
+        u_bank = [psum.tile([P, n, M], F32, name="u%d" % i, tag="u%d" % (i % 3 if i < 4 else 3)) for i, (b, n) in enumerate(GROUPS)]
         warm = keep.tile([P, 1], F32, name="warm")
 
         scale_rows = tab[0, 4 * P * T :].rearrange("(q t) -> q t", t=T).bitcast(I32)
@@ -53,19 +53,21 @@ def tile_list_tabglu_tm_res_kernel(tc, tab, w4_words, w4_scales, w8, r, offs, ou
 
         nc.gpsimd.memset(g4_scales[:], 0)
         nc.vector.memset(tab_scales[:], 0)
-        nc.vector.memset(w8_raw[:, 0, 0:8], 0.0)
         for h in range(2):
-            nc.vector.memset(res[h][:, 0, 0:8], 0.0)
-        nc.vector.memset(warm[:], 0.0)
+            nc.vector.memset(res[h][:], 0.0)
+        nc.vector.memset(tab_words[:, 0:8], 0)
+        nc.vector.memset(w8_raw[:, 0, 0:8], 0.0)
+        nc.gpsimd.memset(warm[:], 0.0)
         nc.scalar.activation(warm[:], warm[:], SILU)
         nc.sync.dma_start(out=lists[:], in_=offs)
-        nc.sync.dma_start(out=tab_words[:], in_=tab[0, : 4 * P * T].rearrange("(p t) -> p t", p=P).bitcast(I32))
         for q in range(4):
             nc.gpsimd.dma_start(out=g4_scales[32 * q : 32 * q + 4, :], in_=w4_rows[4 * q : 4 * q + 4, :])
             nc.sync.dma_start(out=tab_scales[32 * q : 32 * q + 4, :], in_=scale_rows[4 * q : 4 * q + 4, :])
+        nc.sync.dma_start(out=tab_words[:], in_=tab[0, : 4 * P * T].rearrange("(p t) -> p t", p=P).bitcast(I32))
         nc.sync.dma_start(out=w8_raw[:], in_=w8.rearrange("(p j) n -> p j n", j=4))
         nc.sync.dma_start(out=g4_words[:].bitcast(I32), in_=w4_words[0].bitcast(I32))
         for h in range(2):
+            nc.gpsimd.memset(res[h][:, 0, 0:8], 0.0)
             nc.sync.dma_start(out=res[h][:], in_=r[h * 512 : (h + 1) * 512, :].rearrange("(b p) n -> p b n", p=P))
 
         nc.scalar.copy(out=w8_grouped[:], in_=w8_raw[:].rearrange("p j n -> p n j"))
@@ -110,25 +112,31 @@ def tile_list_tabglu_tm_res_kernel(tc, tab, w4_words, w4_scales, w8, r, offs, ou
             first, count = GROUPS[i]
             (engine or nc.sync).dma_start(out=out[first * P : (first + count) * P, :].rearrange("(b p) n -> p b n", p=P), in_=done[i][:])
 
-        gather(0)
         gather_scales(0)
-        multiply(0, True)
+        gather(0)
+        gather(1)
         quantise()
         multiply(0, False)
-        gather_scales(1)
-        multiply(1, True)
+        multiply(0, True)
+        gather(2)
         multiply(1, False)
-        gather_scales(2)
-        for i in (2, 3):
+        multiply(1, True)
+        gather(3)
+        multiply(2, False)
+        multiply(2, True)
+        times(0)
+        plus(0, nc.gpsimd)
+        store(0)
+        for i in (3, 4):
             multiply(i, True)
             multiply(i, False)
-        times(0)
-        plus(0, nc.vector)
-        store(0)
         times(1)
-        plus(1, nc.vector)
+        plus(1, nc.gpsimd)
         store(1)
-        for i in (2, 3):
+        times(2)
+        plus(2, nc.vector)
+        store(2)
+        for i in (3, 4):
             times(i)
             plus(i, nc.vector)
             store(i)

@@ -57,17 +57,19 @@ def tile_list_tabglu_tm_res_kernel(tc, tab, w4_words, w4_scales, w8, r, offs, ou
             nc.vector.memset(res[h][:], 0.0)
         nc.vector.memset(tab_words[:, 0:8], 0)
         nc.vector.memset(w8_raw[:, 0, 0:8], 0.0)
+        nc.vector.memset(g4_scales[:, 0:8], 0)
         nc.gpsimd.memset(warm[:], 0.0)
         nc.scalar.activation(warm[:], warm[:], SILU)
         nc.sync.dma_start(out=lists[:], in_=offs)
         for q in range(4):
-            nc.gpsimd.dma_start(out=g4_scales[32 * q : 32 * q + 4, :], in_=w4_rows[4 * q : 4 * q + 4, :])
             nc.sync.dma_start(out=tab_scales[32 * q : 32 * q + 4, :], in_=scale_rows[4 * q : 4 * q + 4, :])
         nc.sync.dma_start(out=tab_words[:], in_=tab[0, : 4 * P * T].rearrange("(p t) -> p t", p=P).bitcast(I32))
         nc.sync.dma_start(out=w8_raw[:], in_=w8.rearrange("(p j) n -> p j n", j=4))
-        nc.sync.dma_start(out=g4_words[:].bitcast(I32), in_=w4_words[0].bitcast(I32))
+        nc.scalar.dma_start(out=g4_words[:].bitcast(I32), in_=w4_words[0].bitcast(I32))
+        for q in range(4):
+            nc.sync.dma_start(out=g4_scales[32 * q : 32 * q + 4, :], in_=w4_rows[4 * q : 4 * q + 4, :])
         for h in range(2):
-            nc.gpsimd.memset(res[h][:, 0, 0:8], 0.0)
+            nc.vector.memset(res[h][:, 0, 0:8], 0.0)
             nc.sync.dma_start(out=res[h][:], in_=r[h * 512 : (h + 1) * 512, :].rearrange("(b p) n -> p b n", p=P))
 
         nc.scalar.copy(out=w8_grouped[:], in_=w8_raw[:].rearrange("p j n -> p n j"))
@@ -114,19 +116,19 @@ def tile_list_tabglu_tm_res_kernel(tc, tab, w4_words, w4_scales, w8, r, offs, ou
 
         gather_scales(0)
         gather(0)
+        multiply(0, True)
         gather(1)
+        multiply(1, True)
         quantise()
         multiply(0, False)
-        multiply(0, True)
-        gather(2)
         multiply(1, False)
-        multiply(1, True)
-        gather(3)
-        multiply(2, False)
+        gather(2)
         multiply(2, True)
+        multiply(2, False)
         times(0)
         plus(0, nc.gpsimd)
         store(0)
+        gather(3)
         for i in (3, 4):
             multiply(i, True)
             multiply(i, False)

@@ -5,22 +5,27 @@ import concourse.mybir as mybir
 K, M, T, S = 512, 128, 2048, 1024
 FLOPS = 2 * 2 * K * M * S
 
+P = 128
+PACK = 4
+QUADRANTS = 4
+ROWS = 4
+TABLE_WORD_BYTES = PACK * P * T
+GATHER_BLOCKS = 2
+GATHERS = S // (GATHER_BLOCKS * P)
+
+GROUPS = ((0, 2), (2, 2), (4, 2), (6, 1), (7, 1))
+
 F32 = mybir.dt.float32
 BF16 = mybir.dt.bfloat16
 I32 = mybir.dt.int32
 U32 = mybir.dt.uint32
 U16 = mybir.dt.uint16
 U8 = mybir.dt.uint8
-FP8X4 = mybir.dt.float8_e4m3fn_x4
-FP4X4 = mybir.dt.float4_e2m1fn_x4
+E4M3_X4 = mybir.dt.float8_e4m3fn_x4
+E2M1_X4 = mybir.dt.float4_e2m1fn_x4
 SILU = mybir.ActivationFunctionType.Silu
 MULT = mybir.AluOpType.mult
 ADD = mybir.AluOpType.add
-
-P = 128
-PIECES = (2, 2, 2, 2)
-SPIECES = (8,)
-GROUPS = ((0, 2), (2, 2), (4, 2), (6, 1), (7, 1))
 
 
 def tile_list_tabglu_tm_res_kernel(tc, tab, w4_words, w4_scales, w8, r, offs, out):
@@ -32,113 +37,114 @@ def tile_list_tabglu_tm_res_kernel(tc, tab, w4_words, w4_scales, w8, r, offs, ou
         lists = keep.tile([P, S // 16], U16, name="lists")
         tab_words = keep.tile([P, T], I32, name="tab_words", align_bytes=64)
         tab_scales = keep.tile([P, T // 4], I32, name="tab_scales", align_bytes=64)
-        g4_words = keep.tile([P, 2 * M], U8, name="g4_words", align_bytes=64)
-        g4_scales = keep.tile([P, M // 4], I32, name="g4_scales", align_bytes=64)
-        w8_raw = keep.tile([P, 4, M], F32, name="w8_raw", align_bytes=64)
-        w8_grouped = keep.tile([P, M, 4], BF16, name="w8_grouped", align_bytes=64)
+        w4_codes = keep.tile([P, 2 * M], U8, name="w4_codes", align_bytes=64)
+        w4_planes = keep.tile([P, M // 4], I32, name="w4_planes", align_bytes=64)
+        w8_raw = keep.tile([P, PACK, M], F32, name="w8_raw", align_bytes=64)
+        w8_grouped = keep.tile([P, M, PACK], BF16, name="w8_grouped", tag="stage", align_bytes=64)
         w8_codes = keep.tile([P, M], U32, name="w8_codes", align_bytes=64)
-        w8_scales = keep.tile([P, M], U8, name="w8_scales", align_bytes=64)
-        picked_words = [keep.tile([P, n * P], U32, name="pw%d" % i, align_bytes=64) for i, n in enumerate(PIECES)]
-        picked_scales = [keep.tile([P, n * P], U8, name="ps%d" % i, align_bytes=64) for i, n in enumerate(SPIECES)]
-        res = [keep.tile([P, 4, M], F32, name="res%d" % h) for h in range(2)]
-        sil = [keep.tile([P, n, M], F32, name="sil%d" % i) for i, (b, n) in enumerate(GROUPS)]
-        prod = [keep.tile([P, n, M], F32, name="prod%d" % i) for i, (b, n) in enumerate(GROUPS)]
-        done = [keep.tile([P, n, M], F32, name="done%d" % i) for i, (b, n) in enumerate(GROUPS)]
-        e_bank = [psum.tile([P, n, M], F32, name="e%d" % i, tag="e%d" % (i % 3 if i < 4 else 3)) for i, (b, n) in enumerate(GROUPS)]
-        u_bank = [psum.tile([P, n, M], F32, name="u%d" % i, tag="u%d" % (i % 3 if i < 4 else 3)) for i, (b, n) in enumerate(GROUPS)]
-        warm = keep.tile([P, 1], F32, name="warm")
+        w8_planes = keep.tile([P, M], U8, name="w8_planes", align_bytes=64)
+        picked_words = [
+            keep.tile(
+                [P, GATHER_BLOCKS * P],
+                U32,
+                name="picked_words%d" % g,
+                tag="stage" if g == GATHERS - 1 else "picked_words%d" % g,
+                align_bytes=64,
+            )
+            for g in range(GATHERS)
+        ]
+        picked_scales = keep.tile([P, S], U8, name="picked_scales", align_bytes=64)
+        res = keep.tile([P, S // P, M], F32, name="res")
+        gates = [keep.tile([P, n, M], F32, name="gates%d" % i) for i, (b, n) in enumerate(GROUPS)]
+        prods = [keep.tile([P, n, M], F32, name="prods%d" % i) for i, (b, n) in enumerate(GROUPS)]
+        sums = [keep.tile([P, n, M], F32, name="sums%d" % i) for i, (b, n) in enumerate(GROUPS)]
+        banks = (0, 1, 2, 0, 3)
+        e_psum = [psum.tile([P, n, M], F32, name="e%d" % i, tag="e_bank%d" % banks[i]) for i, (b, n) in enumerate(GROUPS)]
+        u_psum = [psum.tile([P, n, M], F32, name="u%d" % i, tag="u_bank%d" % banks[i]) for i, (b, n) in enumerate(GROUPS)]
+        dummy = keep.tile([P, 1], F32, name="dummy")
 
-        scale_rows = tab[0, 4 * P * T :].rearrange("(q t) -> q t", t=T).bitcast(I32)
-        w4_rows = w4_scales[0].bitcast(I32)
+        tab_scale_rows = tab[0, TABLE_WORD_BYTES:].rearrange("(b t) -> b t", t=T).bitcast(I32)
+        w4_scale_rows = w4_scales[0].bitcast(I32)
 
-        nc.gpsimd.memset(g4_scales[:], 0)
+        nc.gpsimd.memset(w4_planes[:], 0)
+        nc.gpsimd.memset(dummy[:], 0.0)
         nc.vector.memset(tab_scales[:], 0)
-        for h in range(2):
-            nc.vector.memset(res[h][:], 0.0)
         nc.vector.memset(tab_words[:, 0:8], 0)
         nc.vector.memset(w8_raw[:, 0, 0:8], 0.0)
-        nc.vector.memset(g4_scales[:, 0:8], 0)
-        nc.gpsimd.memset(warm[:], 0.0)
-        nc.scalar.activation(warm[:], warm[:], SILU)
+
+        nc.scalar.activation(dummy[:], dummy[:], SILU)
+
         nc.sync.dma_start(out=lists[:], in_=offs)
-        for q in range(4):
-            nc.sync.dma_start(out=tab_scales[32 * q : 32 * q + 4, :], in_=scale_rows[4 * q : 4 * q + 4, :])
-        nc.sync.dma_start(out=tab_words[:], in_=tab[0, : 4 * P * T].rearrange("(p t) -> p t", p=P).bitcast(I32))
-        nc.sync.dma_start(out=w8_raw[:], in_=w8.rearrange("(p j) n -> p j n", j=4))
-        nc.scalar.dma_start(out=g4_words[:].bitcast(I32), in_=w4_words[0].bitcast(I32))
-        for q in range(4):
-            nc.sync.dma_start(out=g4_scales[32 * q : 32 * q + 4, :], in_=w4_rows[4 * q : 4 * q + 4, :])
-        for h in range(2):
-            nc.vector.memset(res[h][:, 0, 0:8], 0.0)
-            nc.sync.dma_start(out=res[h][:], in_=r[h * 512 : (h + 1) * 512, :].rearrange("(b p) n -> p b n", p=P))
+        nc.sync.dma_start(out=w4_codes[:].bitcast(I32), in_=w4_words[0].bitcast(I32))
+        for q in range(QUADRANTS):
+            queue = nc.sync if q == 0 else nc.gpsimd
+            queue.dma_start(out=w4_planes[32 * q : 32 * q + ROWS, :], in_=w4_scale_rows[ROWS * q : ROWS * (q + 1), :])
+        for q in range(QUADRANTS):
+            nc.sync.dma_start(out=tab_scales[32 * q : 32 * q + ROWS, :], in_=tab_scale_rows[ROWS * q : ROWS * (q + 1), :])
+        nc.sync.dma_start(out=tab_words[:], in_=tab[0, :TABLE_WORD_BYTES].rearrange("(p t) -> p t", p=P).bitcast(I32))
+        nc.sync.dma_start(out=w8_raw[:], in_=w8.rearrange("(p j) n -> p j n", j=PACK))
+        nc.gpsimd.tensor_copy(out=res[:, 0, 0:1], in_=dummy[:])
+        nc.sync.dma_start(out=res[:], in_=r.rearrange("(b p) n -> p b n", p=P))
+
+        nc.vector.tensor_copy(out=picked_scales[:], in_=tab_scales[:].bitcast(U8).indirect(lists[:]))
 
         nc.scalar.copy(out=w8_grouped[:], in_=w8_raw[:].rearrange("p j n -> p n j"))
 
-        def gather(i):
-            first = sum(PIECES[:i])
-            cols = slice(first * P // 16, (first + PIECES[i]) * P // 16)
-            nc.vector.tensor_copy(out=picked_words[i][:], in_=tab_words[:].bitcast(U32).indirect(lists[:, cols]))
+        def gather(g):
+            width = GATHER_BLOCKS * P // 16
+            offsets = lists[:, g * width : (g + 1) * width]
+            nc.vector.tensor_copy(out=picked_words[g][:], in_=tab_words[:].bitcast(U32).indirect(offsets))
 
-        def gather_scales(i):
-            first = sum(SPIECES[:i])
-            cols = slice(first * P // 16, (first + SPIECES[i]) * P // 16)
-            nc.vector.tensor_copy(out=picked_scales[i][:], in_=tab_scales[:].bitcast(U8).indirect(lists[:, cols]))
+        def quantise_w8():
+            nc.vector.quantize_mx(
+                out=w8_codes[:].bitcast(E4M3_X4),
+                scales=w8_planes[:],
+                in_=w8_grouped[:].rearrange("p n j -> p (n j)"),
+            )
 
-        def quantise():
-            nc.vector.quantize_mx(out=w8_codes[:].bitcast(FP8X4), scales=w8_scales[:], in_=w8_grouped[:].rearrange("p n j -> p (n j)"))
-
-        def multiply(i, gate):
+        def multiply(bank, i, weights, weight_scales):
             first, count = GROUPS[i]
             for b in range(first, first + count):
-                piece = [x for x in range(len(PIECES)) if sum(PIECES[:x]) <= b][-1]
-                at = (b - sum(PIECES[:piece])) * P
-                codes = picked_words[piece][:, at : at + P].bitcast(FP8X4)
-                piece = [x for x in range(len(SPIECES)) if sum(SPIECES[:x]) <= b][-1]
-                at = (b - sum(SPIECES[:piece])) * P
-                scales = picked_scales[piece][:, at : at + P]
-                if gate:
-                    nc.tensor.matmul_mx(out=e_bank[i][:, b - first, :], lhsT=codes, lhsT_scale=scales, rhs=g4_words[:].bitcast(FP4X4), rhs_scale=g4_scales[:].bitcast(U8), start=True, stop=True)
-                else:
-                    nc.tensor.matmul_mx(out=u_bank[i][:, b - first, :], lhsT=codes, lhsT_scale=scales, rhs=w8_codes[:].bitcast(FP8X4), rhs_scale=w8_scales[:], start=True, stop=True)
-            if gate:
-                nc.scalar.activation(sil[i][:], e_bank[i][:], SILU)
+                at = b % GATHER_BLOCKS * P
+                nc.tensor.matmul_mx(
+                    out=bank[:, b - first, :],
+                    lhsT=picked_words[b // GATHER_BLOCKS][:, at : at + P].bitcast(E4M3_X4),
+                    lhsT_scale=picked_scales[:, b * P : (b + 1) * P],
+                    rhs=weights,
+                    rhs_scale=weight_scales,
+                    start=True,
+                    stop=True,
+                )
 
-        def times(i):
-            nc.vector.tensor_tensor(prod[i][:], sil[i][:], u_bank[i][:], MULT)
+        def gate(i):
+            multiply(e_psum[i], i, w4_codes[:].bitcast(E2M1_X4), w4_planes[:].bitcast(U8))
+            nc.scalar.activation(gates[i][:], e_psum[i][:], SILU)
 
-        def plus(i, engine):
+        def up(i):
+            multiply(u_psum[i], i, w8_codes[:].bitcast(E4M3_X4), w8_planes[:])
+
+        def finish(i, adder):
             first, count = GROUPS[i]
-            engine.tensor_tensor(done[i][:], prod[i][:], res[first // 4][:, first % 4 : first % 4 + count, :], ADD)
+            nc.vector.tensor_tensor(prods[i][:], gates[i][:], u_psum[i][:], MULT)
+            adder.tensor_tensor(sums[i][:], prods[i][:], res[:, first : first + count, :], ADD)
+            rows = out[first * P : (first + count) * P, :]
+            nc.sync.dma_start(out=rows.rearrange("(b p) n -> p b n", p=P), in_=sums[i][:])
 
-        def store(i, engine=None):
-            first, count = GROUPS[i]
-            (engine or nc.sync).dma_start(out=out[first * P : (first + count) * P, :].rearrange("(b p) n -> p b n", p=P), in_=done[i][:])
-
-        gather_scales(0)
         gather(0)
-        multiply(0, True)
+        gate(0)
         gather(1)
-        multiply(1, True)
-        quantise()
-        multiply(0, False)
-        multiply(1, False)
+        gate(1)
+        quantise_w8()
+        up(0)
+        up(1)
         gather(2)
-        multiply(2, True)
-        multiply(2, False)
-        times(0)
-        plus(0, nc.gpsimd)
-        store(0)
+        gate(2)
+        up(2)
+        finish(0, nc.gpsimd)
         gather(3)
         for i in (3, 4):
-            multiply(i, True)
-            multiply(i, False)
-        times(1)
-        plus(1, nc.gpsimd)
-        store(1)
-        times(2)
-        plus(2, nc.vector)
-        store(2)
-        for i in (3, 4):
-            times(i)
-            plus(i, nc.vector)
-            store(i)
+            gate(i)
+            up(i)
+        finish(1, nc.gpsimd)
+        for i in (2, 3, 4):
+            finish(i, nc.vector)

from contextlib import ExitStack

import concourse.mybir as mybir

K, M, T, S = 512, 128, 2048, 1024
FLOPS = 2 * 2 * K * M * S

P = 128
PACK = 4
QUADRANTS = 4
ROWS = 4
TABLE_WORD_BYTES = PACK * P * T
GATHER_BLOCKS = 2
GATHERS = S // (GATHER_BLOCKS * P)

GROUPS = ((0, 2), (2, 2), (4, 2), (6, 1), (7, 1))

F32 = mybir.dt.float32
BF16 = mybir.dt.bfloat16
I32 = mybir.dt.int32
U32 = mybir.dt.uint32
U16 = mybir.dt.uint16
U8 = mybir.dt.uint8
E4M3_X4 = mybir.dt.float8_e4m3fn_x4
E2M1_X4 = mybir.dt.float4_e2m1fn_x4
SILU = mybir.ActivationFunctionType.Silu
MULT = mybir.AluOpType.mult
ADD = mybir.AluOpType.add


def tile_list_tabglu_tm_res_kernel(tc, tab, w4_words, w4_scales, w8, r, offs, out):
    nc = tc.nc
    with ExitStack() as ctx:
        keep = ctx.enter_context(tc.tile_pool(name="keep", bufs=1))
        psum = ctx.enter_context(tc.psum_pool(name="psum", bufs=1))

        lists = keep.tile([P, S // 16], U16, name="lists")
        tab_words = keep.tile([P, T], I32, name="tab_words", align_bytes=64)
        tab_scales = keep.tile([P, T // 4], I32, name="tab_scales", align_bytes=64)
        w4_codes = keep.tile([P, 2 * M], U8, name="w4_codes", align_bytes=64)
        w4_planes = keep.tile([P, M // 4], I32, name="w4_planes", align_bytes=64)
        w8_raw = keep.tile([P, PACK, M], F32, name="w8_raw", align_bytes=64)
        w8_grouped = keep.tile([P, M, PACK], BF16, name="w8_grouped", tag="stage", align_bytes=64)
        w8_codes = keep.tile([P, M], U32, name="w8_codes", align_bytes=64)
        w8_planes = keep.tile([P, M], U8, name="w8_planes", align_bytes=64)
        picked_words = [
            keep.tile(
                [P, GATHER_BLOCKS * P],
                U32,
                name="picked_words%d" % g,
                tag="stage" if g == GATHERS - 1 else "picked_words%d" % g,
                align_bytes=64,
            )
            for g in range(GATHERS)
        ]
        picked_scales = keep.tile([P, S], U8, name="picked_scales", align_bytes=64)
        res = keep.tile([P, S // P, M], F32, name="res")
        gates = [keep.tile([P, n, M], F32, name="gates%d" % i) for i, (b, n) in enumerate(GROUPS)]
        prods = [keep.tile([P, n, M], F32, name="prods%d" % i) for i, (b, n) in enumerate(GROUPS)]
        sums = [keep.tile([P, n, M], F32, name="sums%d" % i) for i, (b, n) in enumerate(GROUPS)]
        banks = (0, 1, 2, 0, 3)
        e_psum = [psum.tile([P, n, M], F32, name="e%d" % i, tag="e_bank%d" % banks[i]) for i, (b, n) in enumerate(GROUPS)]
        u_psum = [psum.tile([P, n, M], F32, name="u%d" % i, tag="u_bank%d" % banks[i]) for i, (b, n) in enumerate(GROUPS)]
        dummy = keep.tile([P, 1], F32, name="dummy")

        tab_scale_rows = tab[0, TABLE_WORD_BYTES:].rearrange("(b t) -> b t", t=T).bitcast(I32)
        w4_scale_rows = w4_scales[0].bitcast(I32)

        nc.gpsimd.memset(w4_planes[:], 0)
        nc.gpsimd.memset(dummy[:], 0.0)
        nc.vector.memset(tab_scales[:], 0)
        nc.vector.memset(tab_words[:, 0:8], 0)
        nc.vector.memset(w8_raw[:, 0, 0:8], 0.0)

        nc.scalar.activation(dummy[:], dummy[:], SILU)

        nc.sync.dma_start(out=lists[:], in_=offs)
        nc.sync.dma_start(out=w4_codes[:].bitcast(I32), in_=w4_words[0].bitcast(I32))
        for q in range(QUADRANTS):
            queue = nc.sync if q == 0 else nc.gpsimd
            queue.dma_start(out=w4_planes[32 * q : 32 * q + ROWS, :], in_=w4_scale_rows[ROWS * q : ROWS * (q + 1), :])
        for q in range(QUADRANTS):
            nc.sync.dma_start(out=tab_scales[32 * q : 32 * q + ROWS, :], in_=tab_scale_rows[ROWS * q : ROWS * (q + 1), :])
        nc.sync.dma_start(out=tab_words[:], in_=tab[0, :TABLE_WORD_BYTES].rearrange("(p t) -> p t", p=P).bitcast(I32))
        nc.sync.dma_start(out=w8_raw[:], in_=w8.rearrange("(p j) n -> p j n", j=PACK))
        nc.gpsimd.tensor_copy(out=res[:, 0, 0:1], in_=dummy[:])
        nc.sync.dma_start(out=res[:], in_=r.rearrange("(b p) n -> p b n", p=P))

        nc.vector.tensor_copy(out=picked_scales[:], in_=tab_scales[:].bitcast(U8).indirect(lists[:]))

        nc.scalar.copy(out=w8_grouped[:], in_=w8_raw[:].rearrange("p j n -> p n j"))

        def gather(g):
            width = GATHER_BLOCKS * P // 16
            offsets = lists[:, g * width : (g + 1) * width]
            nc.vector.tensor_copy(out=picked_words[g][:], in_=tab_words[:].bitcast(U32).indirect(offsets))

        def quantise_w8():
            nc.vector.quantize_mx(
                out=w8_codes[:].bitcast(E4M3_X4),
                scales=w8_planes[:],
                in_=w8_grouped[:].rearrange("p n j -> p (n j)"),
            )

        def multiply(bank, i, weights, weight_scales):
            first, count = GROUPS[i]
            for b in range(first, first + count):
                at = b % GATHER_BLOCKS * P
                nc.tensor.matmul_mx(
                    out=bank[:, b - first, :],
                    lhsT=picked_words[b // GATHER_BLOCKS][:, at : at + P].bitcast(E4M3_X4),
                    lhsT_scale=picked_scales[:, b * P : (b + 1) * P],
                    rhs=weights,
                    rhs_scale=weight_scales,
                    start=True,
                    stop=True,
                )

        def gate(i):
            multiply(e_psum[i], i, w4_codes[:].bitcast(E2M1_X4), w4_planes[:].bitcast(U8))
            nc.scalar.activation(gates[i][:], e_psum[i][:], SILU)

        def up(i):
            multiply(u_psum[i], i, w8_codes[:].bitcast(E4M3_X4), w8_planes[:])

        def finish(i, adder):
            first, count = GROUPS[i]
            nc.vector.tensor_tensor(prods[i][:], gates[i][:], u_psum[i][:], MULT)
            adder.tensor_tensor(sums[i][:], prods[i][:], res[:, first : first + count, :], ADD)
            rows = out[first * P : (first + count) * P, :]
            nc.sync.dma_start(out=rows.rearrange("(b p) n -> p b n", p=P), in_=sums[i][:])

        gather(0)
        gate(0)
        gather(1)
        gate(1)
        quantise_w8()
        up(0)
        up(1)
        gather(2)
        gate(2)
        up(2)
        finish(0, nc.gpsimd)
        gather(3)
        for i in (3, 4):
            gate(i)
            up(i)
        finish(1, nc.gpsimd)
        for i in (2, 3, 4):
            finish(i, nc.vector)
